import numpy as np
import ml_dtypes


def mxq(x, axis, fmt="e4m3"):
    dtype, down = {"e4m3": (ml_dtypes.float8_e4m3fn, 7), "e5m2": (ml_dtypes.float8_e5m2, 14)}[fmt]
    v = np.moveaxis(np.asarray(x, np.float32).astype(ml_dtypes.bfloat16).astype(np.float64), axis, -1)
    blocks = v.reshape(v.shape[:-1] + (-1, 32))
    amax = np.abs(blocks).max(-1, keepdims=True)
    byte = np.maximum(np.where(amax > 0, np.frexp(amax)[1] - 1 + 127, 0) - down, 1)
    scale = np.exp2(byte - 127.0)
    codes = (blocks / scale).astype(np.float32).astype(dtype).astype(np.float64)
    return np.moveaxis((codes * scale).reshape(v.shape), -1, axis)


WIDE = False


def mx_kscale(k):
    if not WIDE:
        return np.ones(k)
    levels = np.array([10, -10, 5, -5, 0])
    if k % 512:
        return np.exp2(np.random.permutation(np.resize(levels, k // 32))).repeat(32)
    a = np.empty((k // 512, 16))
    for p in range(k // 512):
        a[p, :8] = np.random.permutation(np.resize(levels, 8))
        for g in range(8):
            far = levels[np.abs(levels - a[p, g]) >= 10]
            a[p, g + 8] = far[np.random.randint(len(far))]
    return np.exp2(a.ravel()).repeat(32)


def f64(x):
    return np.asarray(x).astype(np.float64)


def striped(idx):
    return np.tile(idx.reshape(-1, 16).T, (8, 1)).astype(np.uint16)


def unstriped(offs):
    return offs[:16].T.reshape(-1).astype(np.int64)


K, T, E, C, N = 1024, 1536, 6, 128, 128


def by_expert(wq, xq):
    return np.concatenate([wq[e].T @ xq[:, e * C:(e + 1) * C] for e in range(E)], axis=1)


def setup_inputs():
    n = np.random.standard_normal
    s = mx_kscale(K)[:, None]
    return {
        "xT": (n((K, T)) * s).astype(np.float32),
        "w": (n((E, K, N)) / np.sqrt(K) / s[None]).astype(np.float32),
        "b": (0.3 * n((N, E))).astype(np.float32),
        "gate": np.tile(np.random.uniform(0.2, 1.0, E * C), (N, 1)).astype(np.float32),
        "offs": striped(np.random.permutation(T)[:E * C]),
    }


def reference(xT, w, b, gate, offs):
    idx = unstriped(offs)
    xq = mxq(f64(xT)[:, idx], 0, "e4m3")
    y = by_expert(mxq(f64(w), 1, "e4m3"), xq)
    y = y + np.repeat(f64(b), C, axis=1)
    out = np.zeros((N, T))
    out[:, idx] = f64(gate) * y
    return out

@@ -1,0 +1,120 @@
+from contextlib import ExitStack
+
+import concourse.mybir as mybir
+
+K, T, E, C, N = 1024, 1536, 6, 128, 128
+SLOTS = E * C
+P = 128
+PASS_K = 512
+PASSES = K // PASS_K
+CHUNK = 512
+PAIR = 2 * C
+
+FLOPS = 2 * SLOTS * K * N
+
+F32 = mybir.dt.float32
+BF16 = mybir.dt.bfloat16
+U32 = mybir.dt.uint32
+U16 = mybir.dt.uint16
+U8 = mybir.dt.uint8
+FP8X4 = mybir.dt.float8_e4m3fn_x4
+IDENTITY = mybir.ActivationFunctionType.Identity
+MULT = mybir.AluOpType.mult
+
+
+def tile_routed_moe_kernel(tc, xT, w, b, gate, offs, out):
+    nc = tc.nc
+    with ExitStack() as ctx:
+        keep = ctx.enter_context(tc.tile_pool(name="keep", bufs=1))
+        psum = ctx.enter_context(tc.psum_pool(name="psum", bufs=1))
+
+        offsets = keep.tile([P, SLOTS // 16], U16, name="offsets")
+        nc.sync.dma_start(offsets[:], offs)
+
+        x_rows = xT.rearrange("(g p u i) t -> g u p i t", p=P, u=2, i=2)
+        raws = {}
+        for g in range(PASSES):
+            for u in range(2):
+                for c in range(T // CHUNK):
+                    raw = keep.tile([P, 2, CHUNK], F32, name=f"x_raw_{g}_{u}_{c}")
+                    nc.sync.dma_start(out=raw[:], in_=x_rows[g, u, :, :, c * CHUNK:(c + 1) * CHUNK])
+                    raws[g, u, c] = raw
+
+        bias = keep.tile([P, E], F32, name="bias")
+        nc.sync.dma_start(out=bias[:], in_=b)
+        w_rows = w.rearrange("e (g p j) n -> e p g (j n)", p=P, j=4)
+        w_raws = []
+        gates = keep.tile([P, SLOTS], F32, name="gates")
+        for e in range(E):
+            w_raw = keep.tile([P, PASSES, 4 * N], F32, name=f"w_raw_{e}")
+            nc.sync.dma_start(out=w_raw[:], in_=w_rows[e])
+            w_raws.append(w_raw)
+            if e == 3:
+                nc.sync.dma_start(out=gates[:], in_=gate)
+
+        window = keep.tile([P, T], F32, name="window")
+        nc.vector.memset(window[:], 0.0)
+
+        x_codes, x_scales = [], []
+        for g in range(PASSES):
+            slots = keep.tile([P, SLOTS, 4], BF16, align_bytes=64, name=f"slots_{g}")
+            words_out = slots[:].rearrange("p s k -> p (s k)").bitcast(U32).rearrange("p (s u) -> p s u", u=2)
+            for u in range(2):
+                pairs = keep.tile([P, T, 2], BF16, align_bytes=64, name=f"pairs_{g}_{u}")
+                for c in range(T // CHUNK):
+                    src = raws[g, u, c][:].rearrange("p i t -> p t i")
+                    dst = pairs[:, c * CHUNK:(c + 1) * CHUNK, :]
+                    if c < 2:
+                        nc.scalar.copy(dst, src)
+                    else:
+                        nc.vector.tensor_copy(dst, src)
+                words = pairs[:].rearrange("p t i -> p (t i)").bitcast(U32)
+                nc.vector.tensor_copy(words_out[:, :, u], words.indirect(offsets[:]))
+            codes = keep.tile([P, SLOTS], U32, align_bytes=64, name=f"x_codes_{g}")
+            scales = keep.tile([P, SLOTS], U8, align_bytes=64, name=f"x_scales_{g}")
+            flat = slots[:].rearrange("p s k -> p (s k)")
+            for s0, s1 in ((0, 512), (512, 768)):
+                nc.vector.quantize_mx(
+                    out=codes[:, s0:s1].bitcast(FP8X4),
+                    scales=scales[:, s0:s1],
+                    in_=flat[:, 4 * s0:4 * s1],
+                )
+            x_codes.append(codes)
+            x_scales.append(scales)
+
+        for pair in range(E // 2):
+            y = keep.tile([P, PAIR], F32, name=f"y_{pair}")
+            for half in range(2):
+                e = 2 * pair + half
+                w_grouped = keep.tile([P, PASSES, N, 4], BF16, align_bytes=64, name=f"w_grouped_{e}")
+                for g in range(PASSES):
+                    nc.scalar.copy(
+                        w_grouped[:, g].rearrange("p (c i) j -> p c j i", i=4),
+                        w_raws[e][:, g].rearrange("p (j c i) -> p c j i", j=4, i=4),
+                    )
+                w_codes = keep.tile([P, PASSES * N], U32, align_bytes=64, name=f"w_codes_{e}")
+                w_scales = keep.tile([P, PASSES * N], U8, align_bytes=64, name=f"w_scales_{e}")
+                nc.vector.quantize_mx(
+                    out=w_codes[:].bitcast(FP8X4),
+                    scales=w_scales[:],
+                    in_=w_grouped[:].rearrange("p g n j -> p (g n j)"),
+                )
+                acc = psum.tile([N, C], F32, name=f"acc_{e}")
+                for g in range(PASSES):
+                    nc.tensor.matmul_mx(
+                        out=acc[:],
+                        lhsT=w_codes[:, g * N:(g + 1) * N].bitcast(FP8X4),
+                        lhsT_scale=w_scales[:, g * N:(g + 1) * N],
+                        rhs=x_codes[g][:, e * C:(e + 1) * C].bitcast(FP8X4),
+                        rhs_scale=x_scales[g][:, e * C:(e + 1) * C],
+                        start=(g == 0),
+                        stop=(g == PASSES - 1),
+                    )
+                nc.scalar.activation(y[:, half * C:(half + 1) * C], acc[:], IDENTITY, bias=bias[:, e:e + 1])
+            nc.vector.tensor_tensor(
+                window[:].indirect(offsets[:, pair * PAIR // 16:(pair + 1) * PAIR // 16]),
+                y[:],
+                gates[:, pair * PAIR:(pair + 1) * PAIR],
+                MULT,
+            )
+        nc.sync.dma_start(out=out, in_=window[:])

@@ -7,8 +7,9 @@ SLOTS = E * C
 P = 128
 PASS_K = 512
 PASSES = K // PASS_K
-CHUNK = 512
-PAIR = 2 * C
+HALF = T // 2
+SCALAR_SHARE = (640, 256)
+SLICES = ((0, 512), (512, 768))
 
 FLOPS = 2 * SLOTS * K * N
 
@@ -20,6 +21,7 @@ U8 = mybir.dt.uint8
 FP8X4 = mybir.dt.float8_e4m3fn_x4
 IDENTITY = mybir.ActivationFunctionType.Identity
 MULT = mybir.AluOpType.mult
+ADD = mybir.AluOpType.add
 
 
 def tile_routed_moe_kernel(tc, xT, w, b, gate, offs, out):
@@ -35,22 +37,23 @@ def tile_routed_moe_kernel(tc, xT, w, b, gate, offs, out):
         raws = {}
         for g in range(PASSES):
             for u in range(2):
-                for c in range(T // CHUNK):
-                    raw = keep.tile([P, 2, CHUNK], F32, name=f"x_raw_{g}_{u}_{c}")
-                    nc.sync.dma_start(out=raw[:], in_=x_rows[g, u, :, :, c * CHUNK:(c + 1) * CHUNK])
+                for c in range(2):
+                    raw = keep.tile([P, 2, HALF], F32, name=f"x_raw_{g}_{u}_{c}")
+                    nc.sync.dma_start(out=raw[:], in_=x_rows[g, u, :, :, c * HALF:(c + 1) * HALF])
                     raws[g, u, c] = raw
 
         bias = keep.tile([P, E], F32, name="bias")
-        nc.sync.dma_start(out=bias[:], in_=b)
-        w_rows = w.rearrange("e (g p j) n -> e p g (j n)", p=P, j=4)
+        w_rows = w.rearrange("e (g p j) n -> p e g (j n)", p=P, j=4)
         w_raws = []
         gates = keep.tile([P, SLOTS], F32, name="gates")
         for e in range(E):
             w_raw = keep.tile([P, PASSES, 4 * N], F32, name=f"w_raw_{e}")
-            nc.sync.dma_start(out=w_raw[:], in_=w_rows[e])
+            nc.sync.dma_start(out=w_raw[:], in_=w_rows[:, e])
             w_raws.append(w_raw)
-            if e == 3:
-                nc.sync.dma_start(out=gates[:], in_=gate)
+            if e == 1:
+                nc.sync.dma_start(out=bias[:], in_=b)
+                nc.sync.dma_start(out=gates[:, 0:384], in_=gate[:, 0:384])
+        nc.sync.dma_start(out=gates[:, 384:768], in_=gate[:, 384:768])
 
         window = keep.tile([P, T], F32, name="window")
         nc.vector.memset(window[:], 0.0)
@@ -61,19 +64,19 @@ def tile_routed_moe_kernel(tc, xT, w, b, gate, offs, out):
             words_out = slots[:].rearrange("p s k -> p (s k)").bitcast(U32).rearrange("p (s u) -> p s u", u=2)
             for u in range(2):
                 pairs = keep.tile([P, T, 2], BF16, align_bytes=64, name=f"pairs_{g}_{u}")
-                for c in range(T // CHUNK):
+                for c in range(2):
                     src = raws[g, u, c][:].rearrange("p i t -> p t i")
-                    dst = pairs[:, c * CHUNK:(c + 1) * CHUNK, :]
-                    if c < 2:
-                        nc.scalar.copy(dst, src)
-                    else:
-                        nc.vector.tensor_copy(dst, src)
+                    dst = pairs[:, c * HALF:(c + 1) * HALF, :]
+                    cut = SCALAR_SHARE[c]
+                    nc.scalar.copy(dst[:, :cut], src[:, :cut])
+                    nc.vector.tensor_copy(dst[:, cut:], src[:, cut:])
                 words = pairs[:].rearrange("p t i -> p (t i)").bitcast(U32)
-                nc.vector.tensor_copy(words_out[:, :, u], words.indirect(offsets[:]))
+                for s0, s1 in SLICES:
+                    nc.vector.tensor_copy(words_out[:, s0:s1, u], words.indirect(offsets[:, s0 // 16:s1 // 16]))
             codes = keep.tile([P, SLOTS], U32, align_bytes=64, name=f"x_codes_{g}")
             scales = keep.tile([P, SLOTS], U8, align_bytes=64, name=f"x_scales_{g}")
             flat = slots[:].rearrange("p s k -> p (s k)")
-            for s0, s1 in ((0, 512), (512, 768)):
+            for s0, s1 in SLICES:
                 nc.vector.quantize_mx(
                     out=codes[:, s0:s1].bitcast(FP8X4),
                     scales=scales[:, s0:s1],
@@ -82,39 +85,51 @@ def tile_routed_moe_kernel(tc, xT, w, b, gate, offs, out):
             x_codes.append(codes)
             x_scales.append(scales)
 
-        for pair in range(E // 2):
-            y = keep.tile([P, PAIR], F32, name=f"y_{pair}")
-            for half in range(2):
-                e = 2 * pair + half
-                w_grouped = keep.tile([P, PASSES, N, 4], BF16, align_bytes=64, name=f"w_grouped_{e}")
-                for g in range(PASSES):
-                    nc.scalar.copy(
-                        w_grouped[:, g].rearrange("p (c i) j -> p c j i", i=4),
-                        w_raws[e][:, g].rearrange("p (j c i) -> p c j i", j=4, i=4),
-                    )
-                w_codes = keep.tile([P, PASSES * N], U32, align_bytes=64, name=f"w_codes_{e}")
-                w_scales = keep.tile([P, PASSES * N], U8, align_bytes=64, name=f"w_scales_{e}")
-                nc.vector.quantize_mx(
-                    out=w_codes[:].bitcast(FP8X4),
-                    scales=w_scales[:],
-                    in_=w_grouped[:].rearrange("p g n j -> p (g n j)"),
+        y = keep.tile([P, SLOTS], F32, name="y")
+
+        def expert(e):
+            grouped = keep.tile([P, PASSES, N, 4], BF16, align_bytes=64, name=f"w_grouped_{e}")
+            dst = grouped[:].rearrange("p g (c i) j -> p g c j i", i=4)
+            src = w_raws[e][:].rearrange("p g (j c i) -> p g c j i", j=4, i=4)
+            if e == 0:
+                nc.gpsimd.tensor_scalar(
+                    grouped[:], w_raws[e][:].rearrange("p g (j n) -> p g n j", j=4), 1.0, 0.0, MULT, ADD
                 )
-                acc = psum.tile([N, C], F32, name=f"acc_{e}")
-                for g in range(PASSES):
-                    nc.tensor.matmul_mx(
-                        out=acc[:],
-                        lhsT=w_codes[:, g * N:(g + 1) * N].bitcast(FP8X4),
-                        lhsT_scale=w_scales[:, g * N:(g + 1) * N],
-                        rhs=x_codes[g][:, e * C:(e + 1) * C].bitcast(FP8X4),
-                        rhs_scale=x_scales[g][:, e * C:(e + 1) * C],
-                        start=(g == 0),
-                        stop=(g == PASSES - 1),
-                    )
-                nc.scalar.activation(y[:, half * C:(half + 1) * C], acc[:], IDENTITY, bias=bias[:, e:e + 1])
-            nc.vector.tensor_tensor(
-                window[:].indirect(offsets[:, pair * PAIR // 16:(pair + 1) * PAIR // 16]),
-                y[:],
-                gates[:, pair * PAIR:(pair + 1) * PAIR],
-                MULT,
+            else:
+                nc.scalar.copy(dst, src)
+            w_codes = keep.tile([P, PASSES * N], U32, align_bytes=64, name=f"w_codes_{e}")
+            w_scales = keep.tile([P, PASSES * N], U8, align_bytes=64, name=f"w_scales_{e}")
+            nc.vector.quantize_mx(
+                out=w_codes[:].bitcast(FP8X4),
+                scales=w_scales[:],
+                in_=grouped[:].rearrange("p g n j -> p (g n j)"),
             )
+            acc = psum.tile([N, C], F32, name=f"acc_{e}")
+            for g in range(PASSES):
+                nc.tensor.matmul_mx(
+                    out=acc[:],
+                    lhsT=w_codes[:, g * N:(g + 1) * N].bitcast(FP8X4),
+                    lhsT_scale=w_scales[:, g * N:(g + 1) * N],
+                    rhs=x_codes[g][:, e * C:(e + 1) * C].bitcast(FP8X4),
+                    rhs_scale=x_scales[g][:, e * C:(e + 1) * C],
+                    start=(g == 0),
+                    stop=(g == PASSES - 1),
+                )
+            nc.scalar.activation(y[:, e * C:(e + 1) * C], acc[:], IDENTITY, bias=bias[:, e:e + 1])
+
+        def scatter(s0, s1):
+            nc.vector.tensor_tensor(
+                window[:].indirect(offsets[:, s0 // 16:s1 // 16]), y[:, s0:s1], gates[:, s0:s1], MULT
+            )
+
+        expert(0)
+        expert(1)
+        expert(2)
+        expert(3)
+        scatter(0, 192)
+        scatter(192, 384)
+        expert(4)
+        expert(5)
+        scatter(384, 576)
+        scatter(576, 768)
         nc.sync.dma_start(out=out, in_=window[:])

@@ -8,7 +8,7 @@ P = 128
 PASS_K = 512
 PASSES = K // PASS_K
 HALF = T // 2
-SCALAR_SHARE = (640, 256)
+SCALAR_SHARE = ((384, 384), (704, 448), (704, 448), (640, 256))
 SLICES = ((0, 512), (512, 768))
 
 FLOPS = 2 * SLOTS * K * N
@@ -33,6 +33,14 @@ def tile_routed_moe_kernel(tc, xT, w, b, gate, offs, out):
         offsets = keep.tile([P, SLOTS // 16], U16, name="offsets")
         nc.sync.dma_start(offsets[:], offs)
 
+        w_rows = w.rearrange("e (g p j) n -> p e g (j n)", p=P, j=4)
+        w_raws = []
+
+        def load_weights(e):
+            w_raw = keep.tile([P, PASSES, 4 * N], F32, name=f"w_raw_{e}", tag=f"w_raw_{e}")
+            nc.sync.dma_start(out=w_raw[:], in_=w_rows[:, e])
+            w_raws.append(w_raw)
+
         x_rows = xT.rearrange("(g p u i) t -> g u p i t", p=P, u=2, i=2)
         raws = {}
         for g in range(PASSES):
@@ -43,20 +51,41 @@ def tile_routed_moe_kernel(tc, xT, w, b, gate, offs, out):
                     raws[g, u, c] = raw
 
         bias = keep.tile([P, E], F32, name="bias")
-        w_rows = w.rearrange("e (g p j) n -> p e g (j n)", p=P, j=4)
-        w_raws = []
         gates = keep.tile([P, SLOTS], F32, name="gates")
         for e in range(E):
-            w_raw = keep.tile([P, PASSES, 4 * N], F32, name=f"w_raw_{e}")
-            nc.sync.dma_start(out=w_raw[:], in_=w_rows[:, e])
-            w_raws.append(w_raw)
+            load_weights(e)
             if e == 1:
                 nc.sync.dma_start(out=bias[:], in_=b)
-                nc.sync.dma_start(out=gates[:, 0:384], in_=gate[:, 0:384])
-        nc.sync.dma_start(out=gates[:, 384:768], in_=gate[:, 384:768])
+            if e >= 3:
+                s0, s1 = 256 * (e - 3), 256 * (e - 2)
+                nc.sync.dma_start(out=gates[:, s0:s1], in_=gate[:, s0:s1])
 
         window = keep.tile([P, T], F32, name="window")
         nc.vector.memset(window[:], 0.0)
+
+        w_grouped, w_codes, w_scales = {}, {}, {}
+
+        def interleave_weights(e):
+            grouped = keep.tile([P, PASSES, N, 4], BF16, align_bytes=64, name=f"w_grouped_{e}")
+            dst = grouped[:].rearrange("p g (c i) j -> p g c j i", i=4)
+            src = w_raws[e][:].rearrange("p g (j c i) -> p g c j i", j=4, i=4)
+            if e == 0:
+                nc.gpsimd.tensor_scalar(
+                    grouped[:], w_raws[e][:].rearrange("p g (j n) -> p g n j", j=4), 1.0, 0.0, MULT, ADD
+                )
+            else:
+                nc.scalar.copy(dst, src)
+            w_grouped[e] = grouped
+
+        def quantize_weights(e):
+            codes = keep.tile([P, PASSES * N], U32, align_bytes=64, name=f"w_codes_{e}")
+            scales = keep.tile([P, PASSES * N], U8, align_bytes=64, name=f"w_scales_{e}")
+            nc.vector.quantize_mx(
+                out=codes[:].bitcast(FP8X4),
+                scales=scales[:],
+                in_=w_grouped[e][:].rearrange("p g n j -> p (g n j)"),
+            )
+            w_codes[e], w_scales[e] = codes, scales
 
         x_codes, x_scales = [], []
         for g in range(PASSES):
@@ -67,11 +96,11 @@ def tile_routed_moe_kernel(tc, xT, w, b, gate, offs, out):
                 for c in range(2):
                     src = raws[g, u, c][:].rearrange("p i t -> p t i")
                     dst = pairs[:, c * HALF:(c + 1) * HALF, :]
-                    cut = SCALAR_SHARE[c]
+                    cut = SCALAR_SHARE[2 * g + u][c]
                     nc.scalar.copy(dst[:, :cut], src[:, :cut])
                     nc.vector.tensor_copy(dst[:, cut:], src[:, cut:])
                 words = pairs[:].rearrange("p t i -> p (t i)").bitcast(U32)
-                for s0, s1 in SLICES:
+                for s0, s1 in (SLICES if (g, u) == (1, 1) else ((0, SLOTS),)):
                     nc.vector.tensor_copy(words_out[:, s0:s1, u], words.indirect(offsets[:, s0 // 16:s1 // 16]))
             codes = keep.tile([P, SLOTS], U32, align_bytes=64, name=f"x_codes_{g}")
             scales = keep.tile([P, SLOTS], U8, align_bytes=64, name=f"x_scales_{g}")
@@ -85,51 +114,52 @@ def tile_routed_moe_kernel(tc, xT, w, b, gate, offs, out):
             x_codes.append(codes)
             x_scales.append(scales)
 
-        y = keep.tile([P, SLOTS], F32, name="y")
-
-        def expert(e):
-            grouped = keep.tile([P, PASSES, N, 4], BF16, align_bytes=64, name=f"w_grouped_{e}")
-            dst = grouped[:].rearrange("p g (c i) j -> p g c j i", i=4)
-            src = w_raws[e][:].rearrange("p g (j c i) -> p g c j i", j=4, i=4)
-            if e == 0:
-                nc.gpsimd.tensor_scalar(
-                    grouped[:], w_raws[e][:].rearrange("p g (j n) -> p g n j", j=4), 1.0, 0.0, MULT, ADD
-                )
-            else:
-                nc.scalar.copy(dst, src)
-            w_codes = keep.tile([P, PASSES * N], U32, align_bytes=64, name=f"w_codes_{e}")
-            w_scales = keep.tile([P, PASSES * N], U8, align_bytes=64, name=f"w_scales_{e}")
-            nc.vector.quantize_mx(
-                out=w_codes[:].bitcast(FP8X4),
-                scales=w_scales[:],
-                in_=grouped[:].rearrange("p g n j -> p (g n j)"),
-            )
+        def multiply(e):
             acc = psum.tile([N, C], F32, name=f"acc_{e}")
             for g in range(PASSES):
                 nc.tensor.matmul_mx(
                     out=acc[:],
-                    lhsT=w_codes[:, g * N:(g + 1) * N].bitcast(FP8X4),
-                    lhsT_scale=w_scales[:, g * N:(g + 1) * N],
+                    lhsT=w_codes[e][:, g * N:(g + 1) * N].bitcast(FP8X4),
+                    lhsT_scale=w_scales[e][:, g * N:(g + 1) * N],
                     rhs=x_codes[g][:, e * C:(e + 1) * C].bitcast(FP8X4),
                     rhs_scale=x_scales[g][:, e * C:(e + 1) * C],
                     start=(g == 0),
                     stop=(g == PASSES - 1),
                 )
-            nc.scalar.activation(y[:, e * C:(e + 1) * C], acc[:], IDENTITY, bias=bias[:, e:e + 1])
+            dst = ys[e // 2][:, e % 2 * C:(e % 2 + 1) * C]
+            nc.scalar.activation(dst, acc[:], IDENTITY, bias=bias[:, e:e + 1])
 
-        def scatter(s0, s1):
+        ys = []
+
+        def result_tile(pair, k):
+            y = keep.tile([P, 2 * C], F32, name=f"y_{pair}", tag=f"w_raw_{k}")
+            ys.append(y)
+
+        def scatter(pair):
+            s0, s1 = 2 * C * pair, 2 * C * (pair + 1)
             nc.vector.tensor_tensor(
-                window[:].indirect(offsets[:, s0 // 16:s1 // 16]), y[:, s0:s1], gates[:, s0:s1], MULT
+                window[:].indirect(offsets[:, s0 // 16:s1 // 16]), ys[pair][:], gates[:, s0:s1], MULT
             )
 
-        expert(0)
-        expert(1)
-        expert(2)
-        expert(3)
-        scatter(0, 192)
-        scatter(192, 384)
-        expert(4)
-        expert(5)
-        scatter(384, 576)
-        scatter(576, 768)
+        for e in range(3):
+            interleave_weights(e)
+            quantize_weights(e)
+        result_tile(0, 2)
+        multiply(0)
+        multiply(1)
+        interleave_weights(3)
+        quantize_weights(3)
+        interleave_weights(4)
+        result_tile(1, 4)
+        multiply(2)
+        multiply(3)
+        scatter(0)
+        quantize_weights(4)
+        interleave_weights(5)
+        result_tile(2, 5)
+        multiply(4)
+        scatter(1)
+        quantize_weights(5)
+        multiply(5)
+        scatter(2)
         nc.sync.dma_start(out=out, in_=window[:])

@@ -7,8 +7,12 @@ SLOTS = E * C
 P = 128
 PASS_K = 512
 PASSES = K // PASS_K
-HALF = T // 2
-SCALAR_SHARE = ((384, 384), (704, 448), (704, 448), (640, 256))
+CHUNKS = (
+    ((0, 768, 384), (768, 1536, 256)),
+    ((0, 768, 768), (768, 1536, 256)),
+    ((0, 768, 768), (768, 1536, 256)),
+    ((0, 768, 768), (768, 1280, 128), (1280, 1536, 0)),
+)
 SLICES = ((0, 512), (512, 768))
 
 FLOPS = 2 * SLOTS * K * N
@@ -21,7 +25,6 @@ U8 = mybir.dt.uint8
 FP8X4 = mybir.dt.float8_e4m3fn_x4
 IDENTITY = mybir.ActivationFunctionType.Identity
 MULT = mybir.AluOpType.mult
-ADD = mybir.AluOpType.add
 
 
 def tile_routed_moe_kernel(tc, xT, w, b, gate, offs, out):
@@ -45,10 +48,10 @@ def tile_routed_moe_kernel(tc, xT, w, b, gate, offs, out):
         raws = {}
         for g in range(PASSES):
             for u in range(2):
-                for c in range(2):
-                    raw = keep.tile([P, 2, HALF], F32, name=f"x_raw_{g}_{u}_{c}")
-                    nc.sync.dma_start(out=raw[:], in_=x_rows[g, u, :, :, c * HALF:(c + 1) * HALF])
-                    raws[g, u, c] = raw
+                for t0, t1, cut in CHUNKS[2 * g + u]:
+                    raw = keep.tile([P, 2, t1 - t0], F32, name=f"x_raw_{g}_{u}_{t0}")
+                    nc.sync.dma_start(out=raw[:], in_=x_rows[g, u, :, :, t0:t1])
+                    raws[g, u, t0] = raw
 
         bias = keep.tile([P, E], F32, name="bias")
         gates = keep.tile([P, SLOTS], F32, name="gates")
@@ -56,9 +59,10 @@ def tile_routed_moe_kernel(tc, xT, w, b, gate, offs, out):
             load_weights(e)
             if e == 1:
                 nc.sync.dma_start(out=bias[:], in_=b)
-            if e >= 3:
-                s0, s1 = 256 * (e - 3), 256 * (e - 2)
-                nc.sync.dma_start(out=gates[:, s0:s1], in_=gate[:, s0:s1])
+            if e == 3:
+                nc.sync.dma_start(out=gates[:, 0:192], in_=gate[:, 0:192])
+        for s0, s1 in ((192, 384), (384, 768)):
+            nc.sync.dma_start(out=gates[:, s0:s1], in_=gate[:, s0:s1])
 
         window = keep.tile([P, T], F32, name="window")
         nc.vector.memset(window[:], 0.0)
@@ -69,12 +73,7 @@ def tile_routed_moe_kernel(tc, xT, w, b, gate, offs, out):
             grouped = keep.tile([P, PASSES, N, 4], BF16, align_bytes=64, name=f"w_grouped_{e}")
             dst = grouped[:].rearrange("p g (c i) j -> p g c j i", i=4)
             src = w_raws[e][:].rearrange("p g (j c i) -> p g c j i", j=4, i=4)
-            if e == 0:
-                nc.gpsimd.tensor_scalar(
-                    grouped[:], w_raws[e][:].rearrange("p g (j n) -> p g n j", j=4), 1.0, 0.0, MULT, ADD
-                )
-            else:
-                nc.scalar.copy(dst, src)
+            nc.scalar.copy(dst, src)
             w_grouped[e] = grouped
 
         def quantize_weights(e):
@@ -93,12 +92,13 @@ def tile_routed_moe_kernel(tc, xT, w, b, gate, offs, out):
             words_out = slots[:].rearrange("p s k -> p (s k)").bitcast(U32).rearrange("p (s u) -> p s u", u=2)
             for u in range(2):
                 pairs = keep.tile([P, T, 2], BF16, align_bytes=64, name=f"pairs_{g}_{u}")
-                for c in range(2):
-                    src = raws[g, u, c][:].rearrange("p i t -> p t i")
-                    dst = pairs[:, c * HALF:(c + 1) * HALF, :]
-                    cut = SCALAR_SHARE[2 * g + u][c]
-                    nc.scalar.copy(dst[:, :cut], src[:, :cut])
-                    nc.vector.tensor_copy(dst[:, cut:], src[:, cut:])
+                for t0, t1, cut in CHUNKS[2 * g + u]:
+                    src = raws[g, u, t0][:].rearrange("p i t -> p t i")
+                    dst = pairs[:, t0:t1, :]
+                    if cut > 0:
+                        nc.scalar.copy(dst[:, :cut], src[:, :cut])
+                    if cut < t1 - t0:
+                        nc.vector.tensor_copy(dst[:, cut:], src[:, cut:])
                 words = pairs[:].rearrange("p t i -> p (t i)").bitcast(U32)
                 for s0, s1 in (SLICES if (g, u) == (1, 1) else ((0, SLOTS),)):
                     nc.vector.tensor_copy(words_out[:, s0:s1, u], words.indirect(offsets[:, s0 // 16:s1 // 16]))
@@ -126,40 +126,40 @@ def tile_routed_moe_kernel(tc, xT, w, b, gate, offs, out):
                     start=(g == 0),
                     stop=(g == PASSES - 1),
                 )
-            dst = ys[e // 2][:, e % 2 * C:(e % 2 + 1) * C]
+            dst = ys[e // 3][:, e % 3 * C:(e % 3 + 1) * C]
             nc.scalar.activation(dst, acc[:], IDENTITY, bias=bias[:, e:e + 1])
 
         ys = []
 
-        def result_tile(pair, k):
-            y = keep.tile([P, 2 * C], F32, name=f"y_{pair}", tag=f"w_raw_{k}")
+        def result_tile(k):
+            y = keep.tile([P, 3 * C], F32, name=f"y_{k}", tag=f"w_raw_{k}")
             ys.append(y)
 
-        def scatter(pair):
-            s0, s1 = 2 * C * pair, 2 * C * (pair + 1)
+        def scatter(i):
+            s0, s1 = 192 * i, 192 * (i + 1)
             nc.vector.tensor_tensor(
-                window[:].indirect(offsets[:, s0 // 16:s1 // 16]), ys[pair][:], gates[:, s0:s1], MULT
+                window[:].indirect(offsets[:, s0 // 16:s1 // 16]),
+                ys[i // 2][:, 192 * (i % 2):192 * (i % 2 + 1)],
+                gates[:, s0:s1],
+                MULT,
             )
 
-        for e in range(3):
+        for e in range(4):
             interleave_weights(e)
             quantize_weights(e)
-        result_tile(0, 2)
-        multiply(0)
-        multiply(1)
-        interleave_weights(3)
-        quantize_weights(3)
-        interleave_weights(4)
-        result_tile(1, 4)
-        multiply(2)
-        multiply(3)
+        result_tile(3)
+        for e in range(3):
+            multiply(e)
         scatter(0)
+        interleave_weights(4)
         quantize_weights(4)
         interleave_weights(5)
-        result_tile(2, 5)
-        multiply(4)
+        result_tile(5)
         scatter(1)
+        multiply(3)
+        multiply(4)
         quantize_weights(5)
         multiply(5)
         scatter(2)
+        scatter(3)
         nc.sync.dma_start(out=out, in_=window[:])

@@ -9,9 +9,9 @@ PASS_K = 512
 PASSES = K // PASS_K
 CHUNKS = (
     ((0, 768, 384), (768, 1536, 256)),
-    ((0, 768, 768), (768, 1536, 256)),
-    ((0, 768, 768), (768, 1536, 256)),
-    ((0, 768, 768), (768, 1280, 128), (1280, 1536, 0)),
+    ((0, 768, 768), (768, 1536, 512)),
+    ((0, 768, 768), (768, 1536, 512)),
+    ((0, 768, 768), (768, 1280, 384), (1280, 1536, 0)),
 )
 SLICES = ((0, 512), (512, 768))
 

from contextlib import ExitStack

import concourse.mybir as mybir

K, T, E, C, N = 1024, 1536, 6, 128, 128
SLOTS = E * C
P = 128
PASS_K = 512
PASSES = K // PASS_K
CHUNKS = (
    ((0, 768, 384), (768, 1536, 256)),
    ((0, 768, 768), (768, 1536, 512)),
    ((0, 768, 768), (768, 1536, 512)),
    ((0, 768, 768), (768, 1280, 384), (1280, 1536, 0)),
)
SLICES = ((0, 512), (512, 768))

FLOPS = 2 * SLOTS * K * N

F32 = mybir.dt.float32
BF16 = mybir.dt.bfloat16
U32 = mybir.dt.uint32
U16 = mybir.dt.uint16
U8 = mybir.dt.uint8
FP8X4 = mybir.dt.float8_e4m3fn_x4
IDENTITY = mybir.ActivationFunctionType.Identity
MULT = mybir.AluOpType.mult


def tile_routed_moe_kernel(tc, xT, w, b, gate, offs, out):
    nc = tc.nc
    with ExitStack() as ctx:
        keep = ctx.enter_context(tc.tile_pool(name="keep", bufs=1))
        psum = ctx.enter_context(tc.psum_pool(name="psum", bufs=1))

        offsets = keep.tile([P, SLOTS // 16], U16, name="offsets")
        nc.sync.dma_start(offsets[:], offs)

        w_rows = w.rearrange("e (g p j) n -> p e g (j n)", p=P, j=4)
        w_raws = []

        def load_weights(e):
            w_raw = keep.tile([P, PASSES, 4 * N], F32, name=f"w_raw_{e}", tag=f"w_raw_{e}")
            nc.sync.dma_start(out=w_raw[:], in_=w_rows[:, e])
            w_raws.append(w_raw)

        x_rows = xT.rearrange("(g p u i) t -> g u p i t", p=P, u=2, i=2)
        raws = {}
        for g in range(PASSES):
            for u in range(2):
                for t0, t1, cut in CHUNKS[2 * g + u]:
                    raw = keep.tile([P, 2, t1 - t0], F32, name=f"x_raw_{g}_{u}_{t0}")
                    nc.sync.dma_start(out=raw[:], in_=x_rows[g, u, :, :, t0:t1])
                    raws[g, u, t0] = raw

        bias = keep.tile([P, E], F32, name="bias")
        gates = keep.tile([P, SLOTS], F32, name="gates")
        for e in range(E):
            load_weights(e)
            if e == 1:
                nc.sync.dma_start(out=bias[:], in_=b)
            if e == 3:
                nc.sync.dma_start(out=gates[:, 0:192], in_=gate[:, 0:192])
        for s0, s1 in ((192, 384), (384, 768)):
            nc.sync.dma_start(out=gates[:, s0:s1], in_=gate[:, s0:s1])

        window = keep.tile([P, T], F32, name="window")
        nc.vector.memset(window[:], 0.0)

        w_grouped, w_codes, w_scales = {}, {}, {}

        def interleave_weights(e):
            grouped = keep.tile([P, PASSES, N, 4], BF16, align_bytes=64, name=f"w_grouped_{e}")
            dst = grouped[:].rearrange("p g (c i) j -> p g c j i", i=4)
            src = w_raws[e][:].rearrange("p g (j c i) -> p g c j i", j=4, i=4)
            nc.scalar.copy(dst, src)
            w_grouped[e] = grouped

        def quantize_weights(e):
            codes = keep.tile([P, PASSES * N], U32, align_bytes=64, name=f"w_codes_{e}")
            scales = keep.tile([P, PASSES * N], U8, align_bytes=64, name=f"w_scales_{e}")
            nc.vector.quantize_mx(
                out=codes[:].bitcast(FP8X4),
                scales=scales[:],
                in_=w_grouped[e][:].rearrange("p g n j -> p (g n j)"),
            )
            w_codes[e], w_scales[e] = codes, scales

        x_codes, x_scales = [], []
        for g in range(PASSES):
            slots = keep.tile([P, SLOTS, 4], BF16, align_bytes=64, name=f"slots_{g}")
            words_out = slots[:].rearrange("p s k -> p (s k)").bitcast(U32).rearrange("p (s u) -> p s u", u=2)
            for u in range(2):
                pairs = keep.tile([P, T, 2], BF16, align_bytes=64, name=f"pairs_{g}_{u}")
                for t0, t1, cut in CHUNKS[2 * g + u]:
                    src = raws[g, u, t0][:].rearrange("p i t -> p t i")
                    dst = pairs[:, t0:t1, :]
                    if cut > 0:
                        nc.scalar.copy(dst[:, :cut], src[:, :cut])
                    if cut < t1 - t0:
                        nc.vector.tensor_copy(dst[:, cut:], src[:, cut:])
                words = pairs[:].rearrange("p t i -> p (t i)").bitcast(U32)
                for s0, s1 in (SLICES if (g, u) == (1, 1) else ((0, SLOTS),)):
                    nc.vector.tensor_copy(words_out[:, s0:s1, u], words.indirect(offsets[:, s0 // 16:s1 // 16]))
            codes = keep.tile([P, SLOTS], U32, align_bytes=64, name=f"x_codes_{g}")
            scales = keep.tile([P, SLOTS], U8, align_bytes=64, name=f"x_scales_{g}")
            flat = slots[:].rearrange("p s k -> p (s k)")
            for s0, s1 in SLICES:
                nc.vector.quantize_mx(
                    out=codes[:, s0:s1].bitcast(FP8X4),
                    scales=scales[:, s0:s1],
                    in_=flat[:, 4 * s0:4 * s1],
                )
            x_codes.append(codes)
            x_scales.append(scales)

        def multiply(e):
            acc = psum.tile([N, C], F32, name=f"acc_{e}")
            for g in range(PASSES):
                nc.tensor.matmul_mx(
                    out=acc[:],
                    lhsT=w_codes[e][:, g * N:(g + 1) * N].bitcast(FP8X4),
                    lhsT_scale=w_scales[e][:, g * N:(g + 1) * N],
                    rhs=x_codes[g][:, e * C:(e + 1) * C].bitcast(FP8X4),
                    rhs_scale=x_scales[g][:, e * C:(e + 1) * C],
                    start=(g == 0),
                    stop=(g == PASSES - 1),
                )
            dst = ys[e // 3][:, e % 3 * C:(e % 3 + 1) * C]
            nc.scalar.activation(dst, acc[:], IDENTITY, bias=bias[:, e:e + 1])

        ys = []

        def result_tile(k):
            y = keep.tile([P, 3 * C], F32, name=f"y_{k}", tag=f"w_raw_{k}")
            ys.append(y)

        def scatter(i):
            s0, s1 = 192 * i, 192 * (i + 1)
            nc.vector.tensor_tensor(
                window[:].indirect(offsets[:, s0 // 16:s1 // 16]),
                ys[i // 2][:, 192 * (i % 2):192 * (i % 2 + 1)],
                gates[:, s0:s1],
                MULT,
            )

        for e in range(4):
            interleave_weights(e)
            quantize_weights(e)
        result_tile(3)
        for e in range(3):
            multiply(e)
        scatter(0)
        interleave_weights(4)
        quantize_weights(4)
        interleave_weights(5)
        result_tile(5)
        scatter(1)
        multiply(3)
        multiply(4)
        quantize_weights(5)
        multiply(5)
        scatter(2)
        scatter(3)
        nc.sync.dma_start(out=out, in_=window[:])
